import numpy as np
import ml_dtypes


def mxq(x, axis, fmt="e4m3"):
    dtype, down = {"e4m3": (ml_dtypes.float8_e4m3fn, 7), "e5m2": (ml_dtypes.float8_e5m2, 14)}[fmt]
    v = np.moveaxis(np.asarray(x, np.float32).astype(ml_dtypes.bfloat16).astype(np.float64), axis, -1)
    blocks = v.reshape(v.shape[:-1] + (-1, 32))
    amax = np.abs(blocks).max(-1, keepdims=True)
    byte = np.maximum(np.where(amax > 0, np.frexp(amax)[1] - 1 + 127, 0) - down, 1)
    scale = np.exp2(byte - 127.0)
    codes = (blocks / scale).astype(np.float32).astype(dtype).astype(np.float64)
    return np.moveaxis((codes * scale).reshape(v.shape), -1, axis)


WIDE = False


def mx_kscale(k):
    if not WIDE:
        return np.ones(k)
    levels = np.array([30, -30])
    if k % 512:
        return np.exp2(np.random.permutation(np.resize(levels, k // 32))).repeat(32)
    a = np.empty((k // 512, 16))
    for p in range(k // 512):
        a[p, :8] = np.random.permutation(np.resize(levels, 8))
        for g in range(8):
            far = levels[np.abs(levels - a[p, g]) >= 10]
            a[p, g + 8] = far[np.random.randint(len(far))]
    return np.exp2(a.ravel()).repeat(32)


def f64(x):
    return np.asarray(x).astype(np.float64)


def striped(idx):
    return np.tile(np.asarray(idx).reshape(-1, 16).T, (8, 1)).astype(np.uint16)


def unstriped(offs):
    return offs[:16].T.reshape(-1).astype(np.int64)


E2M1 = np.array([0.0, 0.5, 1.0, 1.5, 2.0, 3.0, 4.0, 6.0, -0.0, -0.5, -1.0, -1.5, -2.0, -3.0, -4.0, -6.0])


def pack_weight(w, fmt):
    k, n = w.shape
    w = f64(np.asarray(w, np.float32).astype(ml_dtypes.bfloat16)).reshape(k // 32, 32, n)
    amax = np.abs(w).max(1)
    if fmt == "e4m3":
        byte = np.frexp(amax)[1] - 1 + 127 - 7
    else:
        mant, ex = np.frexp(amax / 6.0)
        byte = np.where(mant > 0.5, ex, ex - 1) + 127
    byte = np.clip(np.where(amax > 0, byte, 1), 1, 254)
    scaled = (w * np.exp2(127.0 - byte)[:, None, :]).reshape(k, n).astype(np.float32)
    by_word = np.ascontiguousarray(scaled.reshape(k // 512, 128, 4, n).transpose(0, 1, 3, 2))
    if fmt == "e4m3":
        words = by_word.astype(ml_dtypes.float8_e4m3fn).view(np.uint8)
    else:
        c = by_word.astype(ml_dtypes.float4_e2m1fn).view(np.uint8) & 0xF
        words = (c[..., 0::2] | (c[..., 1::2] << 4)).reshape(k // 512, 128, 2 * n)
    return np.ascontiguousarray(words), np.ascontiguousarray(byte.astype(np.uint8).reshape(k // 512, 16, n))


def unpack_weight(words, scales, fmt):
    g, _, n = scales.shape
    words = np.ascontiguousarray(words).reshape(g, 128, n, -1)
    if fmt == "e4m3":
        vals = words.view(ml_dtypes.float8_e4m3fn).astype(np.float64)
    else:
        nib = np.empty((g, 128, n, 4), np.uint8)
        nib[..., 0::2] = words & 0xF
        nib[..., 1::2] = words >> 4
        vals = E2M1[nib]
    vals = vals * np.repeat(np.exp2(scales.astype(np.float64) - 127.0), 8, axis=1)[..., None]
    return vals.transpose(0, 1, 3, 2).reshape(g * 512, n)


K, T, J, S, R, V, N = 1024, 1024, 256, 512, 512, 512, 256


def setup_inputs():
    n = np.random.standard_normal
    idx = np.random.permutation(T)[:J]
    idx2 = np.random.permutation(S)[:J]
    idx3 = np.random.permutation(V)[:J]
    fk = mx_kscale(K)
    fr = mx_kscale(R)
    wp = pack_weight(n((K, R)) * 1 / np.sqrt(K) * fk[:, None] * fr, "e2m1")
    wbp = pack_weight(n((R, N)) * 1 / np.sqrt(R) / fr[:, None], "e4m3")
    return {
        "xa": (n((K, T))).astype(np.float32),
        "xb": (n((K, S))).astype(np.float32),
        "hb": (np.random.uniform(0.2, 0.9, (K, 1))).astype(np.float32),
        "fk": (np.random.uniform(0.5, 2.0, (K, 1)) / fk[:, None]).astype(np.float32),
        "w_words": wp[0],
        "w_scales": wp[1],
        "tb": (n((R, V)) * 0.7 * fr[:, None]).astype(np.float32),
        "wb_words": wbp[0],
        "wb_scales": wbp[1],
        "hi": (np.random.uniform(0.4, 1.2, (N, 1))).astype(np.float32),
        "rw": (np.random.uniform(0.5, 2.0, (1, J))).astype(np.float32),
        "offs": striped(idx),
        "offs2": striped(idx2),
        "offs3": striped(idx3),
    }


def reference(xa, xb, hb, fk, w_words, w_scales, tb, wb_words, wb_scales, hi, rw, offs, offs2, offs3):
    idx = unstriped(offs)
    idx2 = unstriped(offs2)
    idx3 = unstriped(offs3)
    wu = unpack_weight(w_words, w_scales, "e2m1")
    wbu = unpack_weight(wb_words, wb_scales, "e4m3")
    u = (f64(xa)[:, idx] - np.minimum(f64(xb)[:, idx2], f64(hb))) * f64(fk)
    uq = mxq(u, 0, "e4m3")
    a = wu.T @ uq
    hid = np.maximum(a, f64(tb)[:, idx3])
    hidq = mxq(hid, 0, "e5m2")
    p = wbu.T @ hidq
    y = np.minimum(p - f64(hi), 0.0) * f64(rw)
    return y

@@ -1,0 +1,254 @@
+from contextlib import ExitStack
+
+import concourse.mybir as mybir
+from concourse.masks import make_identity
+
+K, T, J, S, R, V, N = 1024, 1024, 256, 512, 512, 512, 256
+FLOPS = 2 * K * R * J + 2 * R * N * J
+
+F32 = mybir.dt.float32
+BF16 = mybir.dt.bfloat16
+I32 = mybir.dt.int32
+U32 = mybir.dt.uint32
+U16 = mybir.dt.uint16
+U8 = mybir.dt.uint8
+E4M3 = mybir.dt.float8_e4m3fn_x4
+E5M2 = mybir.dt.float8_e5m2_x4
+E2M1 = mybir.dt.float4_e2m1fn_x4
+ALU = mybir.AluOpType
+ACT = mybir.ActivationFunctionType
+
+P = 128
+PACK = 4
+PASSES = K // (P * PACK)
+PLANES = PASSES * PACK
+HALF = J // 2
+LIST_COLS = J // 16
+N_TILES = N // P
+XB_RUNS = [(0, 1), (2, 3), (4, 5), (6,), (7,)]
+
+
+def tile_list_boundedgaps_abovetable_capped_kernel(
+    tc, xa, xb, hb, fk, w_words, w_scales, tb, wb_words, wb_scales, hi, rw, offs, offs2, offs3, out
+):
+    nc = tc.nc
+    with ExitStack() as ctx:
+        keep = ctx.enter_context(tc.tile_pool(name="keep", bufs=1))
+        psum = ctx.enter_context(tc.psum_pool(name="psum", bufs=1))
+
+        list_a = keep.tile([P, LIST_COLS], U16, name="list_a")
+        list_b = keep.tile([P, LIST_COLS], U16, name="list_b")
+        list_t = keep.tile([P, LIST_COLS], U16, name="list_t")
+        xa_sb = [keep.tile([P, T], F32, name=f"xa{g}") for g in range(PLANES)]
+        xb_sb = [keep.tile([P, len(run), S], F32, name=f"xb{run[0]}") for run in XB_RUNS]
+        xb_plane = [xb_sb[e][:, i, :] for e, run in enumerate(XB_RUNS) for i in range(len(run))]
+        tb_sb = [keep.tile([P, V], F32, name=f"tb{t}") for t in range(PACK)]
+        hb_sb = keep.tile([P, PASSES, PACK], F32, name="hb_sb")
+        fk_sb = keep.tile([P, PASSES, PACK], F32, name="fk_sb")
+        hi_sb = keep.tile([P, N_TILES], F32, name="hi_sb")
+        rw_sb = keep.tile([P, 2], F32, name="rw_sb")
+        w_raw = keep.tile([P, PASSES, 2 * R], U8, name="w_raw", align_bytes=64)
+        ws_raw = keep.tile([P, PASSES, R], U8, name="ws_raw", align_bytes=64)
+        w_dealt = keep.tile([P, PASSES, 2 * R], U8, name="w_dealt", align_bytes=64)
+        ws_dealt = keep.tile([P, PASSES, R], U8, name="ws_dealt", align_bytes=64)
+        wb_sb = keep.tile([P, N], U32, name="wb_sb", align_bytes=64)
+        wbs_sb = keep.tile([P, N], U8, name="wbs_sb", align_bytes=64)
+        ident = keep.tile([P, P], F32, name="ident")
+
+        nc.vector.memset(ws_raw[:].bitcast(I32), 0)
+        nc.vector.memset(wbs_sb[:].bitcast(I32), 0)
+        make_identity(nc, ident[:])
+
+        xa_rows = xa.rearrange("(a p i) t -> a i p t", p=P, i=PACK)
+        xb_rows = xb.rearrange("(a p i) s -> a p i s", p=P, i=PACK)
+        tb_rows = tb.rearrange("(p i) v -> i p v", i=PACK)
+        ws_rows = w_scales.bitcast(I32)
+        wbs_rows = wb_scales.bitcast(I32)
+
+        def load_xa(g):
+            nc.sync.dma_start(xa_sb[g][:], xa_rows[g // PACK, g % PACK])
+
+        def load_xb(e):
+            a, i = divmod(XB_RUNS[e][0], PACK)
+            nc.sync.dma_start(xb_sb[e][:], xb_rows[a, :, i : i + len(XB_RUNS[e]), :])
+
+        def load_ws(q):
+            nc.sync.dma_start(
+                ws_raw[32 * q : 32 * q + 4].bitcast(I32),
+                ws_rows[:, 4 * q : 4 * q + 4, :].rearrange("z r c -> r z c"),
+            )
+
+        def load_wbs(q):
+            nc.sync.dma_start(wbs_sb[32 * q : 32 * q + 4].bitcast(I32), wbs_rows[0, 4 * q : 4 * q + 4, :])
+
+        load_xb(0)
+        nc.sync.dma_start(list_b[:], offs2)
+        nc.sync.dma_start(list_a[:], offs)
+        load_xa(0)
+        nc.sync.dma_start(hb_sb[:], hb.rearrange("(a p i) o -> p a (i o)", p=P, i=PACK))
+        nc.sync.dma_start(fk_sb[:], fk.rearrange("(a p i) o -> p a (i o)", p=P, i=PACK))
+        load_xa(1)
+        nc.sync.dma_start(w_raw[:].bitcast(I32), w_words.bitcast(I32).rearrange("z p c -> p z c"))
+        load_xb(1)
+        load_ws(0)
+        load_ws(1)
+        load_xa(2)
+        load_ws(2)
+        load_ws(3)
+        load_xa(3)
+        load_xb(2)
+        nc.sync.dma_start(list_t[:], offs3)
+        load_xa(4)
+        with nc.allow_non_contiguous_dma(reason="one value a partition"):
+            nc.sync.dma_start(rw_sb[:], rw.rearrange("o (h p) -> p (o h)", p=P))
+            nc.sync.dma_start(hi_sb[:], hi.rearrange("(t p) o -> p (t o)", p=P))
+        load_xa(5)
+        load_xb(3)
+        load_wbs(0)
+        load_wbs(1)
+        load_xa(6)
+        load_wbs(2)
+        load_xb(4)
+        load_wbs(3)
+        load_xa(7)
+        for t in range(PACK):
+            nc.sync.dma_start(tb_sb[t][:], tb_rows[t])
+        nc.sync.dma_start(wb_sb[:].bitcast(I32), wb_words[0].rearrange("p n t -> p (n t)").bitcast(I32))
+
+        ga = keep.tile([P, PLANES, HALF], F32, name="ga")
+        capped = keep.tile([P, PLANES, HALF], F32, name="capped")
+        gb = keep.tile([P, PLANES, J], F32, name="gb")
+        gap = keep.tile([P, PLANES, J], F32, name="gap")
+        gt = keep.tile([P, 2, PACK, HALF], F32, name="gt")
+        u_bf = [keep.tile([P, J, PACK], BF16, name=f"u_bf{a}", align_bytes=64) for a in range(PASSES)]
+        u_codes = [keep.tile([P, J], U32, name=f"u_codes{a}", align_bytes=64) for a in range(PASSES)]
+        u_scales = [keep.tile([P, J], U8, name=f"u_scales{a}", align_bytes=64) for a in range(PASSES)]
+        acc = [psum.tile([P, PACK, HALF], F32, name=f"acc{h}") for h in range(2)]
+        prod = [psum.tile([P, N_TILES, HALF], F32, name=f"prod{h}") for h in range(2)]
+        rw_ps = psum.tile([P, 2, HALF], F32, name="rw_ps")
+
+        def cols(h):
+            return slice(h * HALF, (h + 1) * HALF)
+
+        def list_half(lst, h):
+            return lst[:, h * LIST_COLS // 2 : (h + 1) * LIST_COLS // 2]
+
+        def gather_b(g):
+            nc.scalar.activation(gb[:, g, :], xb_plane[g].indirect(list_b[:]), ACT.Copy)
+
+        def scale_round(g, js, sign):
+            a, i = divmod(g, PACK)
+            nc.vector.tensor_scalar(
+                u_bf[a][:, js, i], gap[:, g, js], fk_sb[:, a, i : i + 1], sign, ALU.mult, ALU.mult
+            )
+
+        def min_minus(g, js):
+            a, i = divmod(g, PACK)
+            nc.vector.scalar_tensor_tensor(
+                gap[:, g, js], gb[:, g, js], hb_sb[:, a, i : i + 1], ga[:, g, :], ALU.min, ALU.subtract
+            )
+
+        def quantize_u(a, js):
+            nc.vector.quantize_mx(
+                u_codes[a][:, js].bitcast(E4M3),
+                u_scales[a][:, js],
+                u_bf[a][:, js, :].rearrange("p j i -> p (j i)"),
+            )
+
+        def first_product(a, h):
+            for t in range(PACK):
+                nc.tensor.matmul_mx(
+                    acc[h][:, t, :],
+                    lhsT=w_dealt[:, a, 2 * P * t : 2 * P * (t + 1)].bitcast(E2M1),
+                    lhsT_scale=ws_dealt[:, a, P * t : P * (t + 1)],
+                    rhs=u_codes[a][:, cols(h)].bitcast(E4M3),
+                    rhs_scale=u_scales[a][:, cols(h)],
+                    start=(a == 0 and t == 0),
+                    stop=(a == PASSES - 1 and t == PACK - 1),
+                )
+
+        every = slice(0, J)
+        for g in range(PLANES):
+            a, i = divmod(g, PACK)
+            gather_b(g)
+            nc.vector.tensor_scalar(capped[:, g, :], gb[:, g, cols(0)], hb_sb[:, a, i : i + 1], None, ALU.min)
+            nc.vector.tensor_tensor(
+                gap[:, g, cols(0)], xa_sb[g][:].indirect(list_half(list_a, 0)), capped[:, g, :], ALU.subtract
+            )
+            nc.scalar.activation(ga[:, g, :], xa_sb[g][:].indirect(list_half(list_a, 1)), ACT.Copy)
+            min_minus(g, cols(1))
+            scale_round(g, cols(0), 1.0)
+            scale_round(g, cols(1), -1.0)
+            if g == 1:
+                nc.vector.tensor_copy(
+                    w_dealt[:].bitcast(U16).rearrange("p z (t m) -> p z t m", t=PACK),
+                    w_raw[:].bitcast(U16).rearrange("p z (m t) -> p z t m", t=PACK),
+                )
+            if g == 2:
+                nc.vector.tensor_copy(
+                    ws_dealt[:].rearrange("p z (t m) -> p z t m", t=PACK),
+                    ws_raw[:].rearrange("p z (m t) -> p z t m", t=PACK),
+                )
+            if g == PACK - 1:
+                quantize_u(0, every)
+                for h in range(2):
+                    first_product(0, h)
+            if g == PACK:
+                for h in range(2):
+                    nc.tensor.transpose(rw_ps[:, h, :], rw_sb[:, h : h + 1].to_broadcast([P, P]), ident[:])
+
+        for h in range(2):
+            quantize_u(PASSES - 1, cols(h))
+        for h in range(2):
+            first_product(PASSES - 1, h)
+
+        for t in range(PACK):
+            for h in range(2):
+                looked_up = tb_sb[t][:].indirect(list_half(list_t, h))
+                if t >= PACK - 2 and h == 0:
+                    nc.vector.tensor_copy(gt[:, h, t, :], looked_up)
+                else:
+                    nc.scalar.activation(gt[:, h, t, :], looked_up, ACT.Copy)
+
+        hid = [keep.tile([P, HALF, PACK], BF16, name=f"hid{h}", align_bytes=64) for h in range(2)]
+        h_codes = [keep.tile([P, HALF], U32, name=f"h_codes{h}", align_bytes=64) for h in range(2)]
+        h_scales = [keep.tile([P, HALF], U8, name=f"h_scales{h}", align_bytes=64) for h in range(2)]
+        short = [keep.tile([P, N_TILES, HALF], F32, name=f"short{h}") for h in range(2)]
+        res = [keep.tile([P, N_TILES, HALF], F32, name=f"res{h}") for h in range(2)]
+        for h in range(2):
+            nc.vector.tensor_tensor(
+                hid[h][:].rearrange("p (c i) t -> p c t i", i=4),
+                acc[h][:].rearrange("p t (c i) -> p c t i", i=4),
+                gt[:, h].rearrange("p t (c i) -> p c t i", i=4),
+                ALU.max,
+            )
+        for h in range(2):
+            nc.vector.quantize_mx(
+                h_codes[h][:].bitcast(E5M2), h_scales[h][:], hid[h][:].rearrange("p j t -> p (j t)")
+            )
+        out_rows = out.rearrange("(t p) j -> p t j", p=P)
+        for h in range(2):
+            for t in range(N_TILES):
+                nc.tensor.matmul_mx(
+                    prod[h][:, t, :],
+                    lhsT=wb_sb[:, P * t : P * (t + 1)].bitcast(E4M3),
+                    lhsT_scale=wbs_sb[:, P * t : P * (t + 1)],
+                    rhs=h_codes[h][:].bitcast(E5M2),
+                    rhs_scale=h_scales[h][:],
+                    start=True,
+                    stop=True,
+                )
+        for h in range(2):
+            for t in range(N_TILES):
+                nc.scalar.activation(
+                    short[h][:, t, :], prod[h][:, t, :], ACT.Relu, bias=hi_sb[:, t : t + 1], scale=-1.0
+                )
+            nc.vector.scalar_tensor_tensor(
+                res[h][:],
+                short[h][:],
+                -1.0,
+                rw_ps[:, h, :].unsqueeze(1).to_broadcast([P, N_TILES, HALF]),
+                ALU.mult,
+                ALU.mult,
+            )
+            nc.sync.dma_start(out_rows[:, :, cols(h)], res[h][:])

@@ -25,7 +25,8 @@ PLANES = PASSES * PACK
 HALF = J // 2
 LIST_COLS = J // 16
 N_TILES = N // P
-XB_RUNS = [(0, 1), (2, 3), (4, 5), (6,), (7,)]
+FUSED = [0, 0, 0, 0, 0, 0, 0, HALF]
+XB_RUNS = [(0, 1), (2, 3), (4,), (5,), (6,), (7,)]
 
 
 def tile_list_boundedgaps_abovetable_capped_kernel(
@@ -81,50 +82,40 @@ def tile_list_boundedgaps_abovetable_capped_kernel(
         def load_wbs(q):
             nc.sync.dma_start(wbs_sb[32 * q : 32 * q + 4].bitcast(I32), wbs_rows[0, 4 * q : 4 * q + 4, :])
 
+        nc.sync.dma_start(w_raw[:].bitcast(I32), w_words.bitcast(I32).rearrange("z p c -> p z c"))
         load_xb(0)
         nc.sync.dma_start(list_b[:], offs2)
         nc.sync.dma_start(list_a[:], offs)
         load_xa(0)
         nc.sync.dma_start(hb_sb[:], hb.rearrange("(a p i) o -> p a (i o)", p=P, i=PACK))
         nc.sync.dma_start(fk_sb[:], fk.rearrange("(a p i) o -> p a (i o)", p=P, i=PACK))
-        load_xa(1)
-        nc.sync.dma_start(w_raw[:].bitcast(I32), w_words.bitcast(I32).rearrange("z p c -> p z c"))
-        load_xb(1)
         load_ws(0)
+        load_xa(1)
+        load_xb(1)
         load_ws(1)
-        load_xa(2)
         load_ws(2)
+        load_xa(2)
         load_ws(3)
-        load_xa(3)
-        load_xb(2)
-        nc.sync.dma_start(list_t[:], offs3)
-        load_xa(4)
         with nc.allow_non_contiguous_dma(reason="one value a partition"):
             nc.sync.dma_start(rw_sb[:], rw.rearrange("o (h p) -> p (o h)", p=P))
-            nc.sync.dma_start(hi_sb[:], hi.rearrange("(t p) o -> p (t o)", p=P))
-        load_xa(5)
-        load_xb(3)
-        load_wbs(0)
-        load_wbs(1)
-        load_xa(6)
-        load_wbs(2)
-        load_xb(4)
-        load_wbs(3)
-        load_xa(7)
+        load_xa(3)
+        nc.sync.dma_start(list_t[:], offs3)
+        for g in range(PACK, PLANES):
+            load_xb(g - 2)
+            load_xa(g)
         for t in range(PACK):
             nc.sync.dma_start(tb_sb[t][:], tb_rows[t])
         nc.sync.dma_start(wb_sb[:].bitcast(I32), wb_words[0].rearrange("p n t -> p (n t)").bitcast(I32))
+        for q in range(4):
+            load_wbs(q)
+        with nc.allow_non_contiguous_dma(reason="one value a partition"):
+            nc.sync.dma_start(hi_sb[:], hi.rearrange("(t p) o -> p (t o)", p=P))
 
-        ga = keep.tile([P, PLANES, HALF], F32, name="ga")
-        capped = keep.tile([P, PLANES, HALF], F32, name="capped")
-        gb = keep.tile([P, PLANES, J], F32, name="gb")
-        gap = keep.tile([P, PLANES, J], F32, name="gap")
-        gt = keep.tile([P, 2, PACK, HALF], F32, name="gt")
-        u_bf = [keep.tile([P, J, PACK], BF16, name=f"u_bf{a}", align_bytes=64) for a in range(PASSES)]
+        u_bf = [keep.tile([P, J, PACK], BF16, name=f"u_bf{a}", tag=f"u_bf{a}", align_bytes=64) for a in range(PASSES)]
         u_codes = [keep.tile([P, J], U32, name=f"u_codes{a}", align_bytes=64) for a in range(PASSES)]
         u_scales = [keep.tile([P, J], U8, name=f"u_scales{a}", align_bytes=64) for a in range(PASSES)]
         acc = [psum.tile([P, PACK, HALF], F32, name=f"acc{h}") for h in range(2)]
-        prod = [psum.tile([P, N_TILES, HALF], F32, name=f"prod{h}") for h in range(2)]
+        prod = [[psum.tile([P, HALF], F32, name=f"prod{h}_{t}") for t in range(N_TILES)] for h in range(2)]
         rw_ps = psum.tile([P, 2, HALF], F32, name="rw_ps")
 
         def cols(h):
@@ -132,21 +123,6 @@ def tile_list_boundedgaps_abovetable_capped_kernel(
 
         def list_half(lst, h):
             return lst[:, h * LIST_COLS // 2 : (h + 1) * LIST_COLS // 2]
-
-        def gather_b(g):
-            nc.scalar.activation(gb[:, g, :], xb_plane[g].indirect(list_b[:]), ACT.Copy)
-
-        def scale_round(g, js, sign):
-            a, i = divmod(g, PACK)
-            nc.vector.tensor_scalar(
-                u_bf[a][:, js, i], gap[:, g, js], fk_sb[:, a, i : i + 1], sign, ALU.mult, ALU.mult
-            )
-
-        def min_minus(g, js):
-            a, i = divmod(g, PACK)
-            nc.vector.scalar_tensor_tensor(
-                gap[:, g, js], gb[:, g, js], hb_sb[:, a, i : i + 1], ga[:, g, :], ALU.min, ALU.subtract
-            )
 
         def quantize_u(a, js):
             nc.vector.quantize_mx(
@@ -167,24 +143,35 @@ def tile_list_boundedgaps_abovetable_capped_kernel(
                     stop=(a == PASSES - 1 and t == PACK - 1),
                 )
 
+        nc.vector.tensor_copy(
+            w_dealt[:].bitcast(U16).rearrange("p z (t m) -> p z t m", t=PACK),
+            w_raw[:].bitcast(U16).rearrange("p z (m t) -> p z t m", t=PACK),
+        )
         every = slice(0, J)
         for g in range(PLANES):
             a, i = divmod(g, PACK)
-            gather_b(g)
-            nc.vector.tensor_scalar(capped[:, g, :], gb[:, g, cols(0)], hb_sb[:, a, i : i + 1], None, ALU.min)
-            nc.vector.tensor_tensor(
-                gap[:, g, cols(0)], xa_sb[g][:].indirect(list_half(list_a, 0)), capped[:, g, :], ALU.subtract
-            )
-            nc.scalar.activation(ga[:, g, :], xa_sb[g][:].indirect(list_half(list_a, 1)), ACT.Copy)
-            min_minus(g, cols(1))
-            scale_round(g, cols(0), 1.0)
-            scale_round(g, cols(1), -1.0)
-            if g == 1:
-                nc.vector.tensor_copy(
-                    w_dealt[:].bitcast(U16).rearrange("p z (t m) -> p z t m", t=PACK),
-                    w_raw[:].bitcast(U16).rearrange("p z (m t) -> p z t m", t=PACK),
+            bound, factor = hb_sb[:, a, i : i + 1], fk_sb[:, a, i : i + 1]
+            gb = keep.tile([P, J], F32, name=f"gb{g}")
+            gap = keep.tile([P, J], F32, name=f"gap{g}")
+            fused, rest = slice(0, FUSED[g]), slice(FUSED[g], J)
+            if FUSED[g] > 0:
+                nc.scalar.activation(gb[:, fused], xb_plane[g].indirect(list_b[:, : FUSED[g] // 16]), ACT.Copy)
+            nc.scalar.activation(gb[:, rest], xb_plane[g].indirect(list_b[:, FUSED[g] // 16 :]), ACT.Copy)
+            if FUSED[g] > 0:
+                capped = keep.tile([P, FUSED[g]], F32, name=f"capped{g}")
+                nc.vector.tensor_scalar(capped[:], gb[:, fused], bound, None, ALU.min)
+                nc.vector.tensor_tensor(
+                    gap[:, fused], xa_sb[g][:].indirect(list_a[:, : FUSED[g] // 16]), capped[:], ALU.subtract
                 )
-            if g == 2:
+            if FUSED[g] < J:
+                ga = keep.tile([P, J - FUSED[g]], F32, name=f"ga{g}")
+                nc.scalar.activation(ga[:], xa_sb[g][:].indirect(list_a[:, FUSED[g] // 16 :]), ACT.Copy)
+                nc.vector.scalar_tensor_tensor(gap[:, rest], gb[:, rest], bound, ga[:], ALU.min, ALU.subtract)
+            if FUSED[g] > 0:
+                nc.vector.tensor_scalar(u_bf[a][:, fused, i], gap[:, fused], factor, None, ALU.mult)
+            if FUSED[g] < J:
+                nc.vector.tensor_scalar(u_bf[a][:, rest, i], gap[:, rest], factor, -1.0, ALU.mult, ALU.mult)
+            if g == 1:
                 nc.vector.tensor_copy(
                     ws_dealt[:].rearrange("p z (t m) -> p z t m", t=PACK),
                     ws_raw[:].rearrange("p z (m t) -> p z t m", t=PACK),
@@ -193,7 +180,6 @@ def tile_list_boundedgaps_abovetable_capped_kernel(
                 quantize_u(0, every)
                 for h in range(2):
                     first_product(0, h)
-            if g == PACK:
                 for h in range(2):
                     nc.tensor.transpose(rw_ps[:, h, :], rw_sb[:, h : h + 1].to_broadcast([P, P]), ident[:])
 
@@ -202,13 +188,11 @@ def tile_list_boundedgaps_abovetable_capped_kernel(
         for h in range(2):
             first_product(PASSES - 1, h)
 
-        for t in range(PACK):
-            for h in range(2):
-                looked_up = tb_sb[t][:].indirect(list_half(list_t, h))
-                if t >= PACK - 2 and h == 0:
-                    nc.vector.tensor_copy(gt[:, h, t, :], looked_up)
-                else:
-                    nc.scalar.activation(gt[:, h, t, :], looked_up, ACT.Copy)
+        gt = keep.tile([P, PACK, J], F32, name="gt")
+        for t in range(PACK - 1):
+            nc.scalar.activation(gt[:, t, :], tb_sb[t][:].indirect(list_t[:]), ACT.Copy)
+        for h in range(2):
+            nc.scalar.activation(gt[:, PACK - 1, cols(h)], tb_sb[PACK - 1][:].indirect(list_half(list_t, h)), ACT.Copy)
 
         hid = [keep.tile([P, HALF, PACK], BF16, name=f"hid{h}", align_bytes=64) for h in range(2)]
         h_codes = [keep.tile([P, HALF], U32, name=f"h_codes{h}", align_bytes=64) for h in range(2)]
@@ -219,7 +203,7 @@ def tile_list_boundedgaps_abovetable_capped_kernel(
             nc.vector.tensor_tensor(
                 hid[h][:].rearrange("p (c i) t -> p c t i", i=4),
                 acc[h][:].rearrange("p t (c i) -> p c t i", i=4),
-                gt[:, h].rearrange("p t (c i) -> p c t i", i=4),
+                gt[:, :, cols(h)].rearrange("p t (c i) -> p c t i", i=4),
                 ALU.max,
             )
         for h in range(2):
@@ -230,7 +214,7 @@ def tile_list_boundedgaps_abovetable_capped_kernel(
         for h in range(2):
             for t in range(N_TILES):
                 nc.tensor.matmul_mx(
-                    prod[h][:, t, :],
+                    prod[h][t][:],
                     lhsT=wb_sb[:, P * t : P * (t + 1)].bitcast(E4M3),
                     lhsT_scale=wbs_sb[:, P * t : P * (t + 1)],
                     rhs=h_codes[h][:].bitcast(E5M2),
@@ -241,14 +225,9 @@ def tile_list_boundedgaps_abovetable_capped_kernel(
         for h in range(2):
             for t in range(N_TILES):
                 nc.scalar.activation(
-                    short[h][:, t, :], prod[h][:, t, :], ACT.Relu, bias=hi_sb[:, t : t + 1], scale=-1.0
+                    short[h][:, t, :], prod[h][t][:], ACT.Relu, bias=hi_sb[:, t : t + 1], scale=-1.0
                 )
-            nc.vector.scalar_tensor_tensor(
-                res[h][:],
-                short[h][:],
-                -1.0,
-                rw_ps[:, h, :].unsqueeze(1).to_broadcast([P, N_TILES, HALF]),
-                ALU.mult,
-                ALU.mult,
-            )
-            nc.sync.dma_start(out_rows[:, :, cols(h)], res[h][:])
+                nc.vector.scalar_tensor_tensor(
+                    res[h][:, t, :], short[h][:, t, :], -1.0, rw_ps[:, h, :], ALU.mult, ALU.mult
+                )
+                nc.sync.dma_start(out_rows[:, t, cols(h)], res[h][:, t, :])

@@ -26,7 +26,7 @@ HALF = J // 2
 LIST_COLS = J // 16
 N_TILES = N // P
 FUSED = [0, 0, 0, 0, 0, 0, 0, HALF]
-XB_RUNS = [(0, 1), (2, 3), (4,), (5,), (6,), (7,)]
+XB_RUNS = [(0, 1), (2, 3), (4, 5), (6,), (7,)]
 
 
 def tile_list_boundedgaps_abovetable_capped_kernel(
@@ -44,10 +44,10 @@ def tile_list_boundedgaps_abovetable_capped_kernel(
         xb_sb = [keep.tile([P, len(run), S], F32, name=f"xb{run[0]}") for run in XB_RUNS]
         xb_plane = [xb_sb[e][:, i, :] for e, run in enumerate(XB_RUNS) for i in range(len(run))]
         tb_sb = [keep.tile([P, V], F32, name=f"tb{t}") for t in range(PACK)]
-        hb_sb = keep.tile([P, PASSES, PACK], F32, name="hb_sb")
-        fk_sb = keep.tile([P, PASSES, PACK], F32, name="fk_sb")
-        hi_sb = keep.tile([P, N_TILES], F32, name="hi_sb")
-        rw_sb = keep.tile([P, 2], F32, name="rw_sb")
+        k_rows = keep.tile([P, P * PACK], F32, name="k_rows")
+        o_rows = keep.tile([P, P], F32, name="o_rows")
+        k_cols = keep.tile([P, PACK, 2 * PASSES], F32, name="k_cols")
+        o_cols = keep.tile([P, 4], F32, name="o_cols")
         w_raw = keep.tile([P, PASSES, 2 * R], U8, name="w_raw", align_bytes=64)
         ws_raw = keep.tile([P, PASSES, R], U8, name="ws_raw", align_bytes=64)
         w_dealt = keep.tile([P, PASSES, 2 * R], U8, name="w_dealt", align_bytes=64)
@@ -58,6 +58,8 @@ def tile_list_boundedgaps_abovetable_capped_kernel(
 
         nc.vector.memset(ws_raw[:].bitcast(I32), 0)
         nc.vector.memset(wbs_sb[:].bitcast(I32), 0)
+        nc.gpsimd.memset(k_rows[:], 0.0)
+        nc.gpsimd.memset(o_rows[:], 0.0)
         make_identity(nc, ident[:])
 
         xa_rows = xa.rearrange("(a p i) t -> a i p t", p=P, i=PACK)
@@ -85,38 +87,44 @@ def tile_list_boundedgaps_abovetable_capped_kernel(
         nc.sync.dma_start(w_raw[:].bitcast(I32), w_words.bitcast(I32).rearrange("z p c -> p z c"))
         load_xb(0)
         nc.sync.dma_start(list_b[:], offs2)
-        nc.sync.dma_start(list_a[:], offs)
         load_xa(0)
-        nc.sync.dma_start(hb_sb[:], hb.rearrange("(a p i) o -> p a (i o)", p=P, i=PACK))
-        nc.sync.dma_start(fk_sb[:], fk.rearrange("(a p i) o -> p a (i o)", p=P, i=PACK))
+        nc.sync.dma_start(k_rows[0:PASSES, :], hb.rearrange("(a c) o -> a (c o)", a=PASSES))
+        nc.sync.dma_start(k_rows[PASSES : 2 * PASSES, :], fk.rearrange("(a c) o -> a (c o)", a=PASSES))
+        nc.sync.dma_start(list_a[:], offs)
         load_ws(0)
         load_xa(1)
         load_xb(1)
         load_ws(1)
-        load_ws(2)
         load_xa(2)
+        load_ws(2)
         load_ws(3)
-        with nc.allow_non_contiguous_dma(reason="one value a partition"):
-            nc.sync.dma_start(rw_sb[:], rw.rearrange("o (h p) -> p (o h)", p=P))
+        nc.sync.dma_start(o_rows[0:2, :], rw.rearrange("o (h c) -> (o h) c", h=2))
         load_xa(3)
+        load_xb(2)
+        nc.sync.dma_start(o_rows[2:4, :], hi.rearrange("(t c) o -> t (c o)", t=N_TILES))
+        load_xa(4)
+        load_xa(5)
+        load_xb(3)
+        load_xa(6)
+        load_xb(4)
+        load_xa(7)
         nc.sync.dma_start(list_t[:], offs3)
-        for g in range(PACK, PLANES):
-            load_xb(g - 2)
-            load_xa(g)
         for t in range(PACK):
             nc.sync.dma_start(tb_sb[t][:], tb_rows[t])
         nc.sync.dma_start(wb_sb[:].bitcast(I32), wb_words[0].rearrange("p n t -> p (n t)").bitcast(I32))
         for q in range(4):
             load_wbs(q)
-        with nc.allow_non_contiguous_dma(reason="one value a partition"):
-            nc.sync.dma_start(hi_sb[:], hi.rearrange("(t p) o -> p (t o)", p=P))
 
         u_bf = [keep.tile([P, J, PACK], BF16, name=f"u_bf{a}", tag=f"u_bf{a}", align_bytes=64) for a in range(PASSES)]
         u_codes = [keep.tile([P, J], U32, name=f"u_codes{a}", align_bytes=64) for a in range(PASSES)]
         u_scales = [keep.tile([P, J], U8, name=f"u_scales{a}", align_bytes=64) for a in range(PASSES)]
         acc = [psum.tile([P, PACK, HALF], F32, name=f"acc{h}") for h in range(2)]
         prod = [[psum.tile([P, HALF], F32, name=f"prod{h}_{t}") for t in range(N_TILES)] for h in range(2)]
-        rw_ps = psum.tile([P, 2, HALF], F32, name="rw_ps")
+        k_ps = psum.tile([P, PACK, P], F32, name="k_ps")
+        o_ps = psum.tile([P, 3, P], F32, name="o_ps")
+        for i in range(PACK):
+            nc.tensor.transpose(k_ps[:, i, :], k_rows[:, i : P * PACK : PACK], ident[:])
+        nc.vector.tensor_copy(k_cols[:], k_ps[:, :, 0 : 2 * PASSES])
 
         def cols(h):
             return slice(h * HALF, (h + 1) * HALF)
@@ -150,7 +158,7 @@ def tile_list_boundedgaps_abovetable_capped_kernel(
         every = slice(0, J)
         for g in range(PLANES):
             a, i = divmod(g, PACK)
-            bound, factor = hb_sb[:, a, i : i + 1], fk_sb[:, a, i : i + 1]
+            bound, factor = k_cols[:, i, a : a + 1], k_cols[:, i, PASSES + a : PASSES + a + 1]
             gb = keep.tile([P, J], F32, name=f"gb{g}")
             gap = keep.tile([P, J], F32, name=f"gap{g}")
             fused, rest = slice(0, FUSED[g]), slice(FUSED[g], J)
@@ -180,8 +188,11 @@ def tile_list_boundedgaps_abovetable_capped_kernel(
                 quantize_u(0, every)
                 for h in range(2):
                     first_product(0, h)
+            if g == PACK:
+                nc.tensor.transpose(o_ps[:, 2, :], o_rows[:], ident[:])
+                nc.vector.tensor_copy(o_cols[:], o_ps[:, 2, 0:4])
                 for h in range(2):
-                    nc.tensor.transpose(rw_ps[:, h, :], rw_sb[:, h : h + 1].to_broadcast([P, P]), ident[:])
+                    nc.tensor.transpose(o_ps[:, h, :], o_cols[:, h : h + 1].to_broadcast([P, P]), ident[:])
 
         for h in range(2):
             quantize_u(PASSES - 1, cols(h))
@@ -225,9 +236,9 @@ def tile_list_boundedgaps_abovetable_capped_kernel(
         for h in range(2):
             for t in range(N_TILES):
                 nc.scalar.activation(
-                    short[h][:, t, :], prod[h][t][:], ACT.Relu, bias=hi_sb[:, t : t + 1], scale=-1.0
+                    short[h][:, t, :], prod[h][t][:], ACT.Relu, bias=o_cols[:, 2 + t : 3 + t], scale=-1.0
                 )
                 nc.vector.scalar_tensor_tensor(
-                    res[h][:, t, :], short[h][:, t, :], -1.0, rw_ps[:, h, :], ALU.mult, ALU.mult
+                    res[h][:, t, :], short[h][:, t, :], -1.0, o_ps[:, h, :], ALU.mult, ALU.mult
                 )
                 nc.sync.dma_start(out_rows[:, t, cols(h)], res[h][:, t, :])

from contextlib import ExitStack

import concourse.mybir as mybir
from concourse.masks import make_identity

K, T, J, S, R, V, N = 1024, 1024, 256, 512, 512, 512, 256
FLOPS = 2 * K * R * J + 2 * R * N * J

F32 = mybir.dt.float32
BF16 = mybir.dt.bfloat16
I32 = mybir.dt.int32
U32 = mybir.dt.uint32
U16 = mybir.dt.uint16
U8 = mybir.dt.uint8
E4M3 = mybir.dt.float8_e4m3fn_x4
E5M2 = mybir.dt.float8_e5m2_x4
E2M1 = mybir.dt.float4_e2m1fn_x4
ALU = mybir.AluOpType
ACT = mybir.ActivationFunctionType

P = 128
PACK = 4
PASSES = K // (P * PACK)
PLANES = PASSES * PACK
HALF = J // 2
LIST_COLS = J // 16
N_TILES = N // P
FUSED = [0, 0, 0, 0, 0, 0, 0, HALF]
XB_RUNS = [(0, 1), (2, 3), (4, 5), (6,), (7,)]


def tile_list_boundedgaps_abovetable_capped_kernel(
    tc, xa, xb, hb, fk, w_words, w_scales, tb, wb_words, wb_scales, hi, rw, offs, offs2, offs3, out
):
    nc = tc.nc
    with ExitStack() as ctx:
        keep = ctx.enter_context(tc.tile_pool(name="keep", bufs=1))
        psum = ctx.enter_context(tc.psum_pool(name="psum", bufs=1))

        list_a = keep.tile([P, LIST_COLS], U16, name="list_a")
        list_b = keep.tile([P, LIST_COLS], U16, name="list_b")
        list_t = keep.tile([P, LIST_COLS], U16, name="list_t")
        xa_sb = [keep.tile([P, T], F32, name=f"xa{g}") for g in range(PLANES)]
        xb_sb = [keep.tile([P, len(run), S], F32, name=f"xb{run[0]}") for run in XB_RUNS]
        xb_plane = [xb_sb[e][:, i, :] for e, run in enumerate(XB_RUNS) for i in range(len(run))]
        tb_sb = [keep.tile([P, V], F32, name=f"tb{t}") for t in range(PACK)]
        k_rows = keep.tile([P, P * PACK], F32, name="k_rows")
        o_rows = keep.tile([P, P], F32, name="o_rows")
        k_cols = keep.tile([P, PACK, 2 * PASSES], F32, name="k_cols")
        o_cols = keep.tile([P, 4], F32, name="o_cols")
        w_raw = keep.tile([P, PASSES, 2 * R], U8, name="w_raw", align_bytes=64)
        ws_raw = keep.tile([P, PASSES, R], U8, name="ws_raw", align_bytes=64)
        w_dealt = keep.tile([P, PASSES, 2 * R], U8, name="w_dealt", align_bytes=64)
        ws_dealt = keep.tile([P, PASSES, R], U8, name="ws_dealt", align_bytes=64)
        wb_sb = keep.tile([P, N], U32, name="wb_sb", align_bytes=64)
        wbs_sb = keep.tile([P, N], U8, name="wbs_sb", align_bytes=64)
        ident = keep.tile([P, P], F32, name="ident")

        nc.vector.memset(ws_raw[:].bitcast(I32), 0)
        nc.vector.memset(wbs_sb[:].bitcast(I32), 0)
        nc.gpsimd.memset(k_rows[:], 0.0)
        nc.gpsimd.memset(o_rows[:], 0.0)
        make_identity(nc, ident[:])

        xa_rows = xa.rearrange("(a p i) t -> a i p t", p=P, i=PACK)
        xb_rows = xb.rearrange("(a p i) s -> a p i s", p=P, i=PACK)
        tb_rows = tb.rearrange("(p i) v -> i p v", i=PACK)
        ws_rows = w_scales.bitcast(I32)
        wbs_rows = wb_scales.bitcast(I32)

        def load_xa(g):
            nc.sync.dma_start(xa_sb[g][:], xa_rows[g // PACK, g % PACK])

        def load_xb(e):
            a, i = divmod(XB_RUNS[e][0], PACK)
            nc.sync.dma_start(xb_sb[e][:], xb_rows[a, :, i : i + len(XB_RUNS[e]), :])

        def load_ws(q):
            nc.sync.dma_start(
                ws_raw[32 * q : 32 * q + 4].bitcast(I32),
                ws_rows[:, 4 * q : 4 * q + 4, :].rearrange("z r c -> r z c"),
            )

        def load_wbs(q):
            nc.sync.dma_start(wbs_sb[32 * q : 32 * q + 4].bitcast(I32), wbs_rows[0, 4 * q : 4 * q + 4, :])

        nc.sync.dma_start(w_raw[:].bitcast(I32), w_words.bitcast(I32).rearrange("z p c -> p z c"))
        load_xb(0)
        nc.sync.dma_start(list_b[:], offs2)
        load_xa(0)
        nc.sync.dma_start(k_rows[0:PASSES, :], hb.rearrange("(a c) o -> a (c o)", a=PASSES))
        nc.sync.dma_start(k_rows[PASSES : 2 * PASSES, :], fk.rearrange("(a c) o -> a (c o)", a=PASSES))
        nc.sync.dma_start(list_a[:], offs)
        load_ws(0)
        load_xa(1)
        load_xb(1)
        load_ws(1)
        load_xa(2)
        load_ws(2)
        load_ws(3)
        nc.sync.dma_start(o_rows[0:2, :], rw.rearrange("o (h c) -> (o h) c", h=2))
        load_xa(3)
        load_xb(2)
        nc.sync.dma_start(o_rows[2:4, :], hi.rearrange("(t c) o -> t (c o)", t=N_TILES))
        load_xa(4)
        load_xa(5)
        load_xb(3)
        load_xa(6)
        load_xb(4)
        load_xa(7)
        nc.sync.dma_start(list_t[:], offs3)
        for t in range(PACK):
            nc.sync.dma_start(tb_sb[t][:], tb_rows[t])
        nc.sync.dma_start(wb_sb[:].bitcast(I32), wb_words[0].rearrange("p n t -> p (n t)").bitcast(I32))
        for q in range(4):
            load_wbs(q)

        u_bf = [keep.tile([P, J, PACK], BF16, name=f"u_bf{a}", tag=f"u_bf{a}", align_bytes=64) for a in range(PASSES)]
        u_codes = [keep.tile([P, J], U32, name=f"u_codes{a}", align_bytes=64) for a in range(PASSES)]
        u_scales = [keep.tile([P, J], U8, name=f"u_scales{a}", align_bytes=64) for a in range(PASSES)]
        acc = [psum.tile([P, PACK, HALF], F32, name=f"acc{h}") for h in range(2)]
        prod = [[psum.tile([P, HALF], F32, name=f"prod{h}_{t}") for t in range(N_TILES)] for h in range(2)]
        k_ps = psum.tile([P, PACK, P], F32, name="k_ps")
        o_ps = psum.tile([P, 3, P], F32, name="o_ps")
        for i in range(PACK):
            nc.tensor.transpose(k_ps[:, i, :], k_rows[:, i : P * PACK : PACK], ident[:])
        nc.vector.tensor_copy(k_cols[:], k_ps[:, :, 0 : 2 * PASSES])

        def cols(h):
            return slice(h * HALF, (h + 1) * HALF)

        def list_half(lst, h):
            return lst[:, h * LIST_COLS // 2 : (h + 1) * LIST_COLS // 2]

        def quantize_u(a, js):
            nc.vector.quantize_mx(
                u_codes[a][:, js].bitcast(E4M3),
                u_scales[a][:, js],
                u_bf[a][:, js, :].rearrange("p j i -> p (j i)"),
            )

        def first_product(a, h):
            for t in range(PACK):
                nc.tensor.matmul_mx(
                    acc[h][:, t, :],
                    lhsT=w_dealt[:, a, 2 * P * t : 2 * P * (t + 1)].bitcast(E2M1),
                    lhsT_scale=ws_dealt[:, a, P * t : P * (t + 1)],
                    rhs=u_codes[a][:, cols(h)].bitcast(E4M3),
                    rhs_scale=u_scales[a][:, cols(h)],
                    start=(a == 0 and t == 0),
                    stop=(a == PASSES - 1 and t == PACK - 1),
                )

        nc.vector.tensor_copy(
            w_dealt[:].bitcast(U16).rearrange("p z (t m) -> p z t m", t=PACK),
            w_raw[:].bitcast(U16).rearrange("p z (m t) -> p z t m", t=PACK),
        )
        every = slice(0, J)
        for g in range(PLANES):
            a, i = divmod(g, PACK)
            bound, factor = k_cols[:, i, a : a + 1], k_cols[:, i, PASSES + a : PASSES + a + 1]
            gb = keep.tile([P, J], F32, name=f"gb{g}")
            gap = keep.tile([P, J], F32, name=f"gap{g}")
            fused, rest = slice(0, FUSED[g]), slice(FUSED[g], J)
            if FUSED[g] > 0:
                nc.scalar.activation(gb[:, fused], xb_plane[g].indirect(list_b[:, : FUSED[g] // 16]), ACT.Copy)
            nc.scalar.activation(gb[:, rest], xb_plane[g].indirect(list_b[:, FUSED[g] // 16 :]), ACT.Copy)
            if FUSED[g] > 0:
                capped = keep.tile([P, FUSED[g]], F32, name=f"capped{g}")
                nc.vector.tensor_scalar(capped[:], gb[:, fused], bound, None, ALU.min)
                nc.vector.tensor_tensor(
                    gap[:, fused], xa_sb[g][:].indirect(list_a[:, : FUSED[g] // 16]), capped[:], ALU.subtract
                )
            if FUSED[g] < J:
                ga = keep.tile([P, J - FUSED[g]], F32, name=f"ga{g}")
                nc.scalar.activation(ga[:], xa_sb[g][:].indirect(list_a[:, FUSED[g] // 16 :]), ACT.Copy)
                nc.vector.scalar_tensor_tensor(gap[:, rest], gb[:, rest], bound, ga[:], ALU.min, ALU.subtract)
            if FUSED[g] > 0:
                nc.vector.tensor_scalar(u_bf[a][:, fused, i], gap[:, fused], factor, None, ALU.mult)
            if FUSED[g] < J:
                nc.vector.tensor_scalar(u_bf[a][:, rest, i], gap[:, rest], factor, -1.0, ALU.mult, ALU.mult)
            if g == 1:
                nc.vector.tensor_copy(
                    ws_dealt[:].rearrange("p z (t m) -> p z t m", t=PACK),
                    ws_raw[:].rearrange("p z (m t) -> p z t m", t=PACK),
                )
            if g == PACK - 1:
                quantize_u(0, every)
                for h in range(2):
                    first_product(0, h)
            if g == PACK:
                nc.tensor.transpose(o_ps[:, 2, :], o_rows[:], ident[:])
                nc.vector.tensor_copy(o_cols[:], o_ps[:, 2, 0:4])
                for h in range(2):
                    nc.tensor.transpose(o_ps[:, h, :], o_cols[:, h : h + 1].to_broadcast([P, P]), ident[:])

        for h in range(2):
            quantize_u(PASSES - 1, cols(h))
        for h in range(2):
            first_product(PASSES - 1, h)

        gt = keep.tile([P, PACK, J], F32, name="gt")
        for t in range(PACK - 1):
            nc.scalar.activation(gt[:, t, :], tb_sb[t][:].indirect(list_t[:]), ACT.Copy)
        for h in range(2):
            nc.scalar.activation(gt[:, PACK - 1, cols(h)], tb_sb[PACK - 1][:].indirect(list_half(list_t, h)), ACT.Copy)

        hid = [keep.tile([P, HALF, PACK], BF16, name=f"hid{h}", align_bytes=64) for h in range(2)]
        h_codes = [keep.tile([P, HALF], U32, name=f"h_codes{h}", align_bytes=64) for h in range(2)]
        h_scales = [keep.tile([P, HALF], U8, name=f"h_scales{h}", align_bytes=64) for h in range(2)]
        short = [keep.tile([P, N_TILES, HALF], F32, name=f"short{h}") for h in range(2)]
        res = [keep.tile([P, N_TILES, HALF], F32, name=f"res{h}") for h in range(2)]
        for h in range(2):
            nc.vector.tensor_tensor(
                hid[h][:].rearrange("p (c i) t -> p c t i", i=4),
                acc[h][:].rearrange("p t (c i) -> p c t i", i=4),
                gt[:, :, cols(h)].rearrange("p t (c i) -> p c t i", i=4),
                ALU.max,
            )
        for h in range(2):
            nc.vector.quantize_mx(
                h_codes[h][:].bitcast(E5M2), h_scales[h][:], hid[h][:].rearrange("p j t -> p (j t)")
            )
        out_rows = out.rearrange("(t p) j -> p t j", p=P)
        for h in range(2):
            for t in range(N_TILES):
                nc.tensor.matmul_mx(
                    prod[h][t][:],
                    lhsT=wb_sb[:, P * t : P * (t + 1)].bitcast(E4M3),
                    lhsT_scale=wbs_sb[:, P * t : P * (t + 1)],
                    rhs=h_codes[h][:].bitcast(E5M2),
                    rhs_scale=h_scales[h][:],
                    start=True,
                    stop=True,
                )
        for h in range(2):
            for t in range(N_TILES):
                nc.scalar.activation(
                    short[h][:, t, :], prod[h][t][:], ACT.Relu, bias=o_cols[:, 2 + t : 3 + t], scale=-1.0
                )
                nc.vector.scalar_tensor_tensor(
                    res[h][:, t, :], short[h][:, t, :], -1.0, o_ps[:, h, :], ALU.mult, ALU.mult
                )
                nc.sync.dma_start(out_rows[:, t, cols(h)], res[h][:, t, :])
